import numpy as np
import ml_dtypes


def mxq(x, axis, fmt="e4m3"):
    dtype, down = {"e4m3": (ml_dtypes.float8_e4m3fn, 7), "e5m2": (ml_dtypes.float8_e5m2, 14)}[fmt]
    v = np.moveaxis(np.asarray(x, np.float32).astype(ml_dtypes.bfloat16).astype(np.float64), axis, -1)
    blocks = v.reshape(v.shape[:-1] + (-1, 32))
    amax = np.abs(blocks).max(-1, keepdims=True)
    byte = np.maximum(np.where(amax > 0, np.frexp(amax)[1] - 1 + 127, 0) - down, 1)
    scale = np.exp2(byte - 127.0)
    codes = (blocks / scale).astype(np.float32).astype(dtype).astype(np.float64)
    return np.moveaxis((codes * scale).reshape(v.shape), -1, axis)


WIDE = False


def mx_kscale(k):
    if not WIDE:
        return np.ones(k)
    levels = np.array([10, -10, 5, -5, 0])
    if k % 512:
        return np.exp2(np.random.permutation(np.resize(levels, k // 32))).repeat(32)
    a = np.empty((k // 512, 16))
    for p in range(k // 512):
        a[p, :8] = np.random.permutation(np.resize(levels, 8))
        for g in range(8):
            far = levels[np.abs(levels - a[p, g]) >= 10]
            a[p, g + 8] = far[np.random.randint(len(far))]
    return np.exp2(a.ravel()).repeat(32)


def f64(x):
    return np.asarray(x).astype(np.float64)


def striped(idx):
    return np.tile(idx.reshape(-1, 16).T, (8, 1)).astype(np.uint16)


def unstriped(offs):
    return offs[:16].T.reshape(-1).astype(np.int64)


def striped8(idx):
    return np.concatenate([x.reshape(-1, 16).T for x in idx]).astype(np.uint16)


def runs(offs, k):
    lists = np.stack([offs[16 * r : 16 * r + 16].T.reshape(-1) for r in range(8)]).astype(np.int64)
    return lists[np.arange(k) % 512 // 64]


def pack_weight(w):
    k, n = w.shape
    w = f64(np.asarray(w, np.float32).astype(ml_dtypes.bfloat16)).reshape(k // 32, 32, n)
    amax = np.abs(w).max(1)
    byte = np.clip(np.where(amax > 0, np.frexp(amax)[1] - 1 + 127 - 7, 1), 1, 254)
    scaled = (w * np.exp2(127.0 - byte)[:, None, :]).reshape(k, n).astype(np.float32)
    words = np.ascontiguousarray(scaled.reshape(k // 512, 128, 4, n).transpose(0, 1, 3, 2)).astype(ml_dtypes.float8_e4m3fn).view(np.uint8)
    return words, np.ascontiguousarray(byte.astype(np.uint8).reshape(k // 512, 16, n))


def unpack_weight(words, scales):
    g, p, n, _ = words.shape
    vals = np.ascontiguousarray(words).view(ml_dtypes.float8_e4m3fn).astype(np.float64) * np.repeat(np.exp2(scales.astype(np.float64) - 127.0), 8, axis=1)[..., None]
    return vals.transpose(0, 1, 3, 2).reshape(g * 512, n)

def planes(y):
    n, m = y.shape
    v = y.astype(np.float32).astype(ml_dtypes.bfloat16).astype(np.float64).reshape(n // 32, 32, m)
    top = np.abs(v).max(1)
    byte = np.clip(np.where(top > 0, np.frexp(top)[1] - 1 + 127 - 7, 1), 1, 254)
    codes = (v * np.exp2(127.0 - byte)[:, None, :]).reshape(n, m).astype(np.float32).astype(ml_dtypes.float8_e4m3fn).view(np.uint8)
    words = codes.reshape(n // 512, 128, 4, m).transpose(0, 1, 3, 2)
    return np.ascontiguousarray(words), np.ascontiguousarray(byte.astype(np.uint8).reshape(n // 512, 16, m))


K, T, S, N, H = 512, 2048, 512, 512, 512


def setup_inputs():
    n = np.random.standard_normal
    s = mx_kscale(K)[:, None]
    u = mx_kscale(H)
    packed_xT = pack_weight(n((K, T)) * s)
    packed_w1 = pack_weight(n((K, H)) / np.sqrt(K) / s)
    packed_w2 = pack_weight(n((K, H)) / np.sqrt(K) / s)
    packed_w3 = pack_weight(n((H, N)) / np.sqrt(H) / u[:, None])
    return {
        "x_words": packed_xT[0],
        "x_scales": packed_xT[1],
        "w1_words": packed_w1[0],
        "w1_scales": packed_w1[1],
        "w2_words": packed_w2[0],
        "w2_scales": packed_w2[1],
        "gn": (np.random.uniform(0.5, 1.5, (H, 1)) * u[:, None]).astype(np.float32),
        "w3_words": packed_w3[0],
        "w3_scales": packed_w3[1],
        "offs": striped(np.random.permutation(T)[:S]),
        "two": striped(np.random.permutation(T)[:S]),
        "n1": striped8(np.stack([np.random.permutation(S) for _ in range(8)])),
        "n2": striped8(np.stack([np.random.permutation(S) for _ in range(8)])),
        "n3": striped8(np.stack([np.random.permutation(S) for _ in range(8)])),
        "n4": striped8(np.stack([np.random.permutation(S) for _ in range(8)])),
    }


def reference(x_words, x_scales, w1_words, w1_scales, w2_words, w2_scales, gn, w3_words, w3_scales, offs, two, n1, n2, n3, n4):
    xq = unpack_weight(x_words, x_scales)[:, unstriped(offs)]
    y = unpack_weight(w1_words, w1_scales).T @ xq
    x_two = unpack_weight(x_words, x_scales)[:, unstriped(two)]
    d = unpack_weight(w2_words, w2_scales).T @ x_two
    z = f64(gn) * (y[np.arange(H)[:, None], runs(n1, H)] - (np.tanh(d) * (d[np.arange(H)[:, None], runs(n2, H)])))
    h = unpack_weight(w3_words, w3_scales).T @ mxq(z, 0, "e4m3")
    pa = h[np.arange(N)[:, None], runs(n3, N)]
    pb = h[np.arange(N)[:, None], runs(n4, N)]
    out_0 = np.maximum(np.maximum(h, pa), pb) - (0.5 * (np.minimum(np.minimum(h, pa), pb)))
    return (out_0,) + planes(out_0)

@@ -1,0 +1,210 @@
+from contextlib import ExitStack
+
+import concourse.mybir as mybir
+
+F32 = mybir.dt.float32
+BF16 = mybir.dt.bfloat16
+I32 = mybir.dt.int32
+U32 = mybir.dt.uint32
+U16 = mybir.dt.uint16
+U8 = mybir.dt.uint8
+FP8X4 = mybir.dt.float8_e4m3fn_x4
+ALU = mybir.AluOpType
+ACT = mybir.ActivationFunctionType
+
+P = 128
+PACK = 4
+T, S, H = 2048, 512, 512
+PIECES = ((0, 256), (256, 128), (384, 128))
+FLOPS = 3 * 2 * 512 * 512 * 512
+
+
+def tile_picked_twlsoftbrange_none_po_kernel(
+    tc, x_words, x_scales, w1_words, w1_scales, w2_words, w2_scales, gn, w3_words, w3_scales,
+    offs, two, n1, n2, n3, n4, out_0, out_1, out_2,
+):
+    nc = tc.nc
+    with ExitStack() as ctx:
+        keep = ctx.enter_context(tc.tile_pool(name="keep", bufs=1))
+        psum = ctx.enter_context(tc.psum_pool(name="psum", bufs=1))
+
+        def sb(name, shape, dtype):
+            return keep.tile(shape, dtype, name=name, align_bytes=64)
+
+        def load_list(name, src):
+            tile = keep.tile([P, S // 16], U16, name=name)
+            nc.sync.dma_start(tile[:], src)
+            return tile
+
+        def load_words(name, src, width, queue):
+            tile = sb(name, [P, width], I32)
+            queue.dma_start(tile[:], src[0].rearrange("p n t -> p (n t)").bitcast(I32))
+            return tile
+
+        def load_scales(tile, first, src, queue):
+            for q in range(4):
+                queue.dma_start(tile[32 * q + first : 32 * q + first + 4, :].bitcast(I32), src[0, 4 * q : 4 * q + 4, :].bitcast(I32))
+
+        def zeroed(name, width):
+            tile = sb(name, [P, width], U8)
+            nc.vector.memset(tile[:].bitcast(I32), 0)
+            return tile
+
+        def deal_words(name, raw):
+            tile = sb(name, [P, H], I32)
+            nc.vector.tensor_copy(tile[:].rearrange("p (t c i) -> p c t i", t=PACK, i=4), raw[:].rearrange("p (c i t) -> p c t i", t=PACK, i=4))
+            return tile
+
+        def deal_scales(name, raw):
+            tile = sb(name, [P, H], U8)
+            nc.vector.tensor_copy(tile[:].rearrange("p (t c i) -> p c t i", t=PACK, i=16), raw[:].rearrange("p (c i t) -> p c t i", t=PACK, i=16))
+            return tile
+
+        def pick(name, words, scales, lst):
+            w = sb(name + "_words", [P, S], U32)
+            s = sb(name + "_scales", [P, S], U8)
+            nc.vector.tensor_copy(w[:], words[:].bitcast(U32).indirect(lst[:]))
+            nc.vector.tensor_copy(s[:], scales[:].indirect(lst[:]))
+            return w, s
+
+        def cols(lst, start, width):
+            return lst[:, start // 16 : (start + width) // 16]
+
+        def interleave(engine_copy, dst, src):
+            engine_copy(dst[:].rearrange("p (c i) t -> p c t i", i=4), src[:].rearrange("p t (c i) -> p c t i", i=4))
+
+        xs = zeroed("xs", T)
+        w2s_raw = zeroed("w2s_raw", H)
+        w13s_raw = zeroed("w13s_raw", H)
+
+        xw = load_words("xw", x_words, T, nc.sync)
+        two_l = load_list("two_l", two)
+        load_scales(xs, 0, x_scales, nc.scalar)
+        w2w_raw = load_words("w2w_raw", w2_words, H, nc.sync)
+        offs_l = load_list("offs_l", offs)
+        load_scales(w2s_raw, 0, w2_scales, nc.sync)
+        gain = sb("gain", [P, PACK], F32)
+        nc.sync.dma_start(gain[:], gn.rearrange("(p t) o -> p (t o)", t=PACK))
+        w1w_raw = load_words("w1w_raw", w1_words, H, nc.sync)
+        load_scales(w13s_raw, 0, w1_scales, nc.sync)
+        load_scales(w13s_raw, 4, w3_scales, nc.sync)
+        n2_l = load_list("n2_l", n2)
+        n1_l = load_list("n1_l", n1)
+        w3w_raw = load_words("w3w_raw", w3_words, H, nc.sync)
+        n3_l = load_list("n3_l", n3)
+        n4_l = load_list("n4_l", n4)
+
+        x2w, x2s = pick("x2", xw, xs, two_l)
+        w2w = deal_words("w2w", w2w_raw)
+        w2s = deal_scales("w2s", w2s_raw)
+
+        th, dg, yg = [], [], []
+        for t in range(PACK):
+            bank = psum.tile([P, S], F32, name="d_bank", tag="bank%d" % t)
+            m = slice(P * t, P * (t + 1))
+            nc.tensor.matmul_mx(out=bank[:], lhsT=w2w[:, m].bitcast(FP8X4), lhsT_scale=w2s[:, m],
+                                rhs=x2w[:].bitcast(FP8X4), rhs_scale=x2s[:], start=True, stop=True)
+            th.append(sb("th%d" % t, [P, S], F32))
+            dg.append(sb("dg%d" % t, [P, S], F32))
+            nc.scalar.activation(th[t][:], bank[:], ACT.Tanh)
+            nc.scalar.activation(dg[t][:], bank[:], ACT.Copy, scale=gain[:, t : t + 1])
+
+        x1w, x1s = pick("x1", xw, xs, offs_l)
+        w1w = deal_words("w1w", w1w_raw)
+        w13s = deal_scales("w13s", w13s_raw)
+        for t in range(PACK):
+            bank = psum.tile([P, S], F32, name="y_bank", tag="bank%d" % (PACK + t))
+            m = slice(P * t, P * (t + 1))
+            nc.tensor.matmul_mx(out=bank[:], lhsT=w1w[:, m].bitcast(FP8X4), lhsT_scale=w13s[:, m],
+                                rhs=x1w[:].bitcast(FP8X4), rhs_scale=x1s[:], start=True, stop=True)
+            yg.append(sb("yg%d" % t, [P, S], F32))
+            nc.scalar.activation(yg[t][:], bank[:], ACT.Copy, scale=gain[:, t : t + 1])
+        w3w = deal_words("w3w", w3w_raw)
+
+        prod = []
+        for t in range(PACK):
+            prod.append(sb("prod%d" % t, [P, S], F32))
+            for a in (0, 256):
+                nc.vector.tensor_tensor(prod[t][:, a : a + 256], dg[t][:].indirect(cols(n2_l, a, 256)), th[t][:, a : a + 256], ALU.mult)
+
+        hw = [sb("hw%d" % t, [P, S], F32) for t in range(PACK)]
+        hp = []
+        zb = []
+
+        def z_gathers(c):
+            a, w = PIECES[c]
+            z = sb("z%d" % c, [P, PACK, w], F32)
+            for t in range(PACK):
+                nc.vector.tensor_tensor(z[:, t, :], yg[t][:].indirect(cols(n1_l, a, w)), prod[t][:, a : a + w], ALU.subtract)
+            zb.append(sb("zb%d" % c, [P, w, PACK], BF16))
+            interleave(nc.vector.tensor_copy if c == len(PIECES) - 1 else nc.scalar.copy, zb[c], z)
+
+        def h_product(c):
+            a, w = PIECES[c]
+            zw = sb("zw%d" % c, [P, w], U32)
+            zs = sb("zs%d" % c, [P, w], U8)
+            nc.vector.quantize_mx(out=zw[:].bitcast(FP8X4), scales=zs[:], in_=zb[c][:].rearrange("p n t -> p (n t)"))
+            hp.append(sb("hp%d" % c, [P, PACK, w], F32))
+            per_bank = S // w
+            for t0 in range(0, PACK, per_bank):
+                bank = psum.tile([P, per_bank, w], F32, name="h_bank", tag="bank%d" % ((PACK * a + t0 * w) // S))
+                for t in range(t0, t0 + per_bank):
+                    m = slice(P * t, P * (t + 1))
+                    nc.tensor.matmul_mx(out=bank[:, t - t0, :], lhsT=w3w[:, m].bitcast(FP8X4), lhsT_scale=w13s[4:P, m],
+                                        rhs=zw[:].bitcast(FP8X4), rhs_scale=zs[:], start=True, stop=True)
+                for t in range(t0, t0 + per_bank):
+                    nc.scalar.copy(hw[t][:, a : a + w], bank[:, t - t0, :])
+                nc.scalar.copy(hp[c][:, t0 : t0 + per_bank, :], bank[:])
+
+        z_gathers(0)
+        z_gathers(1)
+        h_product(0)
+        z_gathers(2)
+        h_product(1)
+        h_product(2)
+
+        out_rows = out_0.rearrange("(p t) j -> p t j", t=PACK)
+        out_words = out_1[0].rearrange("p n t -> p (n t)").bitcast(I32)
+        os_ = sb("out_scales", [P, S], U8)
+        us, vs, ob = [], [], []
+
+        def h_gathers(c):
+            a, w = PIECES[c]
+            us.append(sb("u%d" % c, [P, PACK, w], F32))
+            vs.append(sb("v%d" % c, [P, PACK, w], F32))
+            for t in range(PACK):
+                nc.vector.tensor_tensor(us[c][:, t, :], hw[t][:].indirect(cols(n3_l, a, w)), hp[c][:, t, :], ALU.subtract)
+                nc.vector.tensor_tensor(vs[c][:, t, :], hw[t][:].indirect(cols(n4_l, a, w)), hp[c][:, t, :], ALU.subtract)
+
+        def combine(c):
+            a, w = PIECES[c]
+            hi = sb("hi%d" % c, [P, PACK, w], F32)
+            lo = sb("lo%d" % c, [P, PACK, w], F32)
+            mix = sb("mix%d" % c, [P, PACK, w], F32)
+            res = sb("res%d" % c, [P, PACK, w], F32)
+            nc.vector.scalar_tensor_tensor(lo[:], us[c][:], 0.0, vs[c][:], ALU.min, ALU.min)
+            nc.vector.scalar_tensor_tensor(hi[:], us[c][:], 0.0, vs[c][:], ALU.max, ALU.max)
+            nc.vector.tensor_tensor(mix[:], hp[c][:], lo[:], ALU.subtract)
+            nc.vector.scalar_tensor_tensor(res[:], mix[:], 0.5, hi[:], ALU.mult, ALU.add)
+            nc.sync.dma_start(out_rows[:, :, a : a + w], res[:])
+            ob.append(sb("ob%d" % c, [P, w, PACK], BF16))
+            interleave(nc.vector.tensor_copy if c == len(PIECES) - 1 else nc.scalar.copy, ob[c], res)
+
+        def planes(c):
+            a, w = PIECES[c]
+            ow = sb("ow%d" % c, [P, w], U32)
+            nc.vector.quantize_mx(out=ow[:].bitcast(FP8X4), scales=os_[:, a : a + w], in_=ob[c][:].rearrange("p n t -> p (n t)"))
+            nc.sync.dma_start(out_words[:, a : a + w], ow[:].bitcast(I32))
+
+        h_gathers(0)
+        combine(0)
+        h_gathers(1)
+        planes(0)
+        combine(1)
+        h_gathers(2)
+        planes(1)
+        combine(2)
+        planes(2)
+        for q in range(4):
+            queue = nc.scalar if q % 2 else nc.sync
+            queue.dma_start(out_2[0, 4 * q : 4 * q + 4, :].bitcast(I32), os_[32 * q : 32 * q + 4, :].bitcast(I32))

@@ -1,6 +1,7 @@
 from contextlib import ExitStack
 
 import concourse.mybir as mybir
+from concourse.masks import make_identity
 
 F32 = mybir.dt.float32
 BF16 = mybir.dt.bfloat16
@@ -15,7 +16,7 @@ ACT = mybir.ActivationFunctionType
 P = 128
 PACK = 4
 T, S, H = 2048, 512, 512
-PIECES = ((0, 256), (256, 128), (384, 128))
+HALF = S // 2
 FLOPS = 3 * 2 * 512 * 512 * 512
 
 
@@ -28,8 +29,8 @@ def tile_picked_twlsoftbrange_none_po_kernel(
         keep = ctx.enter_context(tc.tile_pool(name="keep", bufs=1))
         psum = ctx.enter_context(tc.psum_pool(name="psum", bufs=1))
 
-        def sb(name, shape, dtype):
-            return keep.tile(shape, dtype, name=name, align_bytes=64)
+        def sb(name, shape, dtype, tag=None):
+            return keep.tile(shape, dtype, name=name, tag=tag or name, align_bytes=64)
 
         def load_list(name, src):
             tile = keep.tile([P, S // 16], U16, name=name)
@@ -47,7 +48,7 @@ def tile_picked_twlsoftbrange_none_po_kernel(
 
         def zeroed(name, width):
             tile = sb(name, [P, width], U8)
-            nc.vector.memset(tile[:].bitcast(I32), 0)
+            nc.gpsimd.memset(tile[:].bitcast(I32), 0)
             return tile
 
         def deal_words(name, raw):
@@ -60,8 +61,8 @@ def tile_picked_twlsoftbrange_none_po_kernel(
             nc.vector.tensor_copy(tile[:].rearrange("p (t c i) -> p c t i", t=PACK, i=16), raw[:].rearrange("p (c i t) -> p c t i", t=PACK, i=16))
             return tile
 
-        def pick(name, words, scales, lst):
-            w = sb(name + "_words", [P, S], U32)
+        def pick(name, words, scales, lst, after=None):
+            w = sb(name + "_words", [P, S], U32, tag=after)
             s = sb(name + "_scales", [P, S], U8)
             nc.vector.tensor_copy(w[:], words[:].bitcast(U32).indirect(lst[:]))
             nc.vector.tensor_copy(s[:], scales[:].indirect(lst[:]))
@@ -77,22 +78,24 @@ def tile_picked_twlsoftbrange_none_po_kernel(
         w2s_raw = zeroed("w2s_raw", H)
         w13s_raw = zeroed("w13s_raw", H)
 
-        xw = load_words("xw", x_words, T, nc.sync)
         two_l = load_list("two_l", two)
-        load_scales(xs, 0, x_scales, nc.scalar)
-        w2w_raw = load_words("w2w_raw", w2_words, H, nc.sync)
+        xw = load_words("xw", x_words, T, nc.scalar)
+        w2w_raw = load_words("w2w_raw", w2_words, H, nc.scalar)
+        load_scales(xs, 0, x_scales, nc.sync)
+        load_scales(w2s_raw, 0, w2_scales, nc.scalar)
         offs_l = load_list("offs_l", offs)
-        load_scales(w2s_raw, 0, w2_scales, nc.sync)
-        gain = sb("gain", [P, PACK], F32)
-        nc.sync.dma_start(gain[:], gn.rearrange("(p t) o -> p (t o)", t=PACK))
-        w1w_raw = load_words("w1w_raw", w1_words, H, nc.sync)
-        load_scales(w13s_raw, 0, w1_scales, nc.sync)
-        load_scales(w13s_raw, 4, w3_scales, nc.sync)
         n2_l = load_list("n2_l", n2)
         n1_l = load_list("n1_l", n1)
-        w3w_raw = load_words("w3w_raw", w3_words, H, nc.sync)
         n3_l = load_list("n3_l", n3)
         n4_l = load_list("n4_l", n4)
+        gain = sb("gain", [P, PACK], F32)
+        nc.gpsimd.dma_start(gain[:], gn.rearrange("(p t) o -> p (t o)", t=PACK))
+        load_scales(w13s_raw, 4, w3_scales, nc.gpsimd)
+        w1w_raw = load_words("w1w_raw", w1_words, H, nc.sync)
+        load_scales(w13s_raw, 0, w1_scales, nc.sync)
+        w3w_raw = load_words("w3w_raw", w3_words, H, nc.sync)
+        ident = sb("ident", [P, P], F32)
+        make_identity(nc, ident[:])
 
         x2w, x2s = pick("x2", xw, xs, two_l)
         w2w = deal_words("w2w", w2w_raw)
@@ -105,11 +108,12 @@ def tile_picked_twlsoftbrange_none_po_kernel(
             nc.tensor.matmul_mx(out=bank[:], lhsT=w2w[:, m].bitcast(FP8X4), lhsT_scale=w2s[:, m],
                                 rhs=x2w[:].bitcast(FP8X4), rhs_scale=x2s[:], start=True, stop=True)
             th.append(sb("th%d" % t, [P, S], F32))
-            dg.append(sb("dg%d" % t, [P, S], F32))
+            dg.append(sb("dg%d" % t, [P, 2 * S], F32))
+            nc.vector.memset(dg[t][:, S:], 0.0)
             nc.scalar.activation(th[t][:], bank[:], ACT.Tanh)
-            nc.scalar.activation(dg[t][:], bank[:], ACT.Copy, scale=gain[:, t : t + 1])
+            nc.scalar.activation(dg[t][:, :S], bank[:], ACT.Copy, scale=gain[:, t : t + 1])
 
-        x1w, x1s = pick("x1", xw, xs, offs_l)
+        x1w, x1s = pick("x1", xw, xs, offs_l, after="w2s_raw")
         w1w = deal_words("w1w", w1w_raw)
         w13s = deal_scales("w13s", w13s_raw)
         for t in range(PACK):
@@ -121,90 +125,123 @@ def tile_picked_twlsoftbrange_none_po_kernel(
             nc.scalar.activation(yg[t][:], bank[:], ACT.Copy, scale=gain[:, t : t + 1])
         w3w = deal_words("w3w", w3w_raw)
 
-        prod = []
-        for t in range(PACK):
-            prod.append(sb("prod%d" % t, [P, S], F32))
-            for a in (0, 256):
-                nc.vector.tensor_tensor(prod[t][:, a : a + 256], dg[t][:].indirect(cols(n2_l, a, 256)), th[t][:, a : a + 256], ALU.mult)
-
         hw = [sb("hw%d" % t, [P, S], F32) for t in range(PACK)]
-        hp = []
-        zb = []
+        hp = sb("hp", [P, PACK, S], F32)
 
-        def z_gathers(c):
-            a, w = PIECES[c]
-            z = sb("z%d" % c, [P, PACK, w], F32)
-            for t in range(PACK):
-                nc.vector.tensor_tensor(z[:, t, :], yg[t][:].indirect(cols(n1_l, a, w)), prod[t][:, a : a + w], ALU.subtract)
-            zb.append(sb("zb%d" % c, [P, w, PACK], BF16))
-            interleave(nc.vector.tensor_copy if c == len(PIECES) - 1 else nc.scalar.copy, zb[c], z)
+        def round_pair(engine_copy, dst, t0, src):
+            engine_copy(dst[:, :, t0 : t0 + 2].rearrange("p (c i) t -> p c i t", i=4), src.rearrange("p t (c i) -> p c i t", i=4))
 
-        def h_product(c):
-            a, w = PIECES[c]
-            zw = sb("zw%d" % c, [P, w], U32)
-            zs = sb("zs%d" % c, [P, w], U8)
-            nc.vector.quantize_mx(out=zw[:].bitcast(FP8X4), scales=zs[:], in_=zb[c][:].rearrange("p n t -> p (n t)"))
-            hp.append(sb("hp%d" % c, [P, PACK, w], F32))
-            per_bank = S // w
-            for t0 in range(0, PACK, per_bank):
-                bank = psum.tile([P, per_bank, w], F32, name="h_bank", tag="bank%d" % ((PACK * a + t0 * w) // S))
-                for t in range(t0, t0 + per_bank):
-                    m = slice(P * t, P * (t + 1))
-                    nc.tensor.matmul_mx(out=bank[:, t - t0, :], lhsT=w3w[:, m].bitcast(FP8X4), lhsT_scale=w13s[4:P, m],
-                                        rhs=zw[:].bitcast(FP8X4), rhs_scale=zs[:], start=True, stop=True)
-                for t in range(t0, t0 + per_bank):
-                    nc.scalar.copy(hw[t][:, a : a + w], bank[:, t - t0, :])
-                nc.scalar.copy(hp[c][:, t0 : t0 + per_bank, :], bank[:])
+        prod = [sb("prod%d" % t, [P, S], F32) for t in range(PACK)]
+        for t in range(PACK):
+            nc.vector.tensor_tensor(prod[t][:], dg[t][:].indirect(n2_l[:]), th[t][:], ALU.mult)
 
-        z_gathers(0)
-        z_gathers(1)
-        h_product(0)
-        z_gathers(2)
-        h_product(1)
-        h_product(2)
+        def z_pair(c, t0, zb, engine_copy, tag):
+            a = HALF * c
+            z = sb("z%d_%d" % (c, t0), [P, 2, HALF], F32, tag=tag)
+            for t in (t0, t0 + 1):
+                nc.vector.tensor_tensor(z[:, t - t0, :], yg[t][:].indirect(cols(n1_l, a, HALF)), prod[t][:, a : a + HALF], ALU.subtract)
+            round_pair(engine_copy, zb, t0, z[:])
+
+        def quantised(c, zb):
+            zw = sb("zw%d" % c, [P, HALF], U32)
+            zs = sb("zs%d" % c, [P, HALF], U8)
+            nc.vector.quantize_mx(out=zw[:].bitcast(FP8X4), scales=zs[:], in_=zb[:].rearrange("p n t -> p (n t)"))
+            return zw, zs
+
+        def h_rows(c, zq, rows, tag):
+            bank = psum.tile([P, len(rows), HALF], F32, name="h_bank", tag=tag)
+            for i, t in enumerate(rows):
+                m = slice(P * t, P * (t + 1))
+                nc.tensor.matmul_mx(out=bank[:, i, :], lhsT=w3w[:, m].bitcast(FP8X4), lhsT_scale=w13s[4:P, m],
+                                    rhs=zq[0][:].bitcast(FP8X4), rhs_scale=zq[1][:], start=True, stop=True)
+            for i, t in enumerate(rows):
+                nc.scalar.copy(hw[t][:, HALF * c : HALF * (c + 1)], bank[:, i, :])
+            return bank
+
+        def h_plain(c, rows, bank):
+            nc.scalar.copy(hp[:, rows[0] : rows[-1] + 1, HALF * c : HALF * (c + 1)], bank[:])
+
+        zb0 = sb("zb0", [P, HALF, PACK], BF16, tag="zb0")
+        zb1 = sb("zb1", [P, HALF, PACK], BF16)
+        z_pair(0, 0, zb0, nc.scalar.copy, "z_low")
+        z_pair(0, 2, zb0, nc.scalar.copy, "z_high")
+        z_pair(1, 0, zb1, nc.scalar.copy, "z_low")
+        zq0 = quantised(0, zb0)
+        z_pair(1, 2, zb1, nc.vector.tensor_copy, "zb0")
+        zq1 = quantised(1, zb1)
+        h_plain(0, (0, 1), h_rows(0, zq0, (0, 1), "bank0"))
+        left = h_rows(0, zq0, (2, 3), "bank1")
+        right = [(rows, h_rows(1, zq1, rows, tag)) for rows, tag in (((0,), "bank2"), ((1,), "bank3"), ((2, 3), "bank4"))]
+        h_plain(0, (2, 3), left)
+        for rows, bank in right:
+            h_plain(1, rows, bank)
 
         out_rows = out_0.rearrange("(p t) j -> p t j", t=PACK)
         out_words = out_1[0].rearrange("p n t -> p (n t)").bitcast(I32)
         os_ = sb("out_scales", [P, S], U8)
-        us, vs, ob = [], [], []
+        ob = [sb("ob%d" % c, [P, HALF, PACK], BF16) for c in range(2)]
 
-        def h_gathers(c):
-            a, w = PIECES[c]
-            us.append(sb("u%d" % c, [P, PACK, w], F32))
-            vs.append(sb("v%d" % c, [P, PACK, w], F32))
-            for t in range(PACK):
-                nc.vector.tensor_tensor(us[c][:, t, :], hw[t][:].indirect(cols(n3_l, a, w)), hp[c][:, t, :], ALU.subtract)
-                nc.vector.tensor_tensor(vs[c][:, t, :], hw[t][:].indirect(cols(n4_l, a, w)), hp[c][:, t, :], ALU.subtract)
+        def extremes(unit):
+            c, t0 = unit // 2, 2 * (unit % 2)
+            a = HALF * c
+            u = sb("u%d" % unit, [P, 2, HALF], F32)
+            v = sb("v%d" % unit, [P, 2, HALF], F32)
+            for t in range(t0, t0 + 2):
+                nc.vector.tensor_tensor(u[:, t - t0, :], hw[t][:].indirect(cols(n3_l, a, HALF)), hp[:, t, a : a + HALF], ALU.subtract)
+                nc.vector.tensor_tensor(v[:, t - t0, :], hw[t][:].indirect(cols(n4_l, a, HALF)), hp[:, t, a : a + HALF], ALU.subtract)
+            lo = sb("lo%d" % unit, [P, 2, HALF], F32)
+            hi = sb("hi%d" % unit, [P, 2, HALF], F32)
+            nc.vector.scalar_tensor_tensor(lo[:], u[:], 0.0, v[:], ALU.min, ALU.min)
+            nc.vector.scalar_tensor_tensor(hi[:], u[:], 0.0, v[:], ALU.max, ALU.max)
+            return lo, hi
 
-        def combine(c):
-            a, w = PIECES[c]
-            hi = sb("hi%d" % c, [P, PACK, w], F32)
-            lo = sb("lo%d" % c, [P, PACK, w], F32)
-            mix = sb("mix%d" % c, [P, PACK, w], F32)
-            res = sb("res%d" % c, [P, PACK, w], F32)
-            nc.vector.scalar_tensor_tensor(lo[:], us[c][:], 0.0, vs[c][:], ALU.min, ALU.min)
-            nc.vector.scalar_tensor_tensor(hi[:], us[c][:], 0.0, vs[c][:], ALU.max, ALU.max)
-            nc.vector.tensor_tensor(mix[:], hp[c][:], lo[:], ALU.subtract)
+        def turn(dst, terms):
+            for i, term in enumerate(terms):
+                nc.tensor.matmul(dst, term, ident[:], start=(i == 0), stop=(i == len(terms) - 1), is_transpose=True)
+
+        def sum_on_tensor(unit, lo, hi):
+            c, t0 = unit // 2, 2 * (unit % 2)
+            a = HALF * c
+            turned = psum.tile([P, 4, P], F32, name="turned", tag="bank%d" % (5 + 2 * (unit % 2)))
+            back = psum.tile([P, 2, HALF], F32, name="back", tag="bank%d" % (6 * (1 - unit % 2)))
+            low = sb("low%d" % unit, [P, 2, HALF], F32, tag="low")
+            nc.scalar.activation(low[:], lo[:], ACT.Copy, scale=-1.0)
+            staged = sb("staged%d" % unit, [P, 4, P], F32)
+            for b in range(4):
+                r, j = b // 2, P * (b % 2)
+                top = hi[:, r, j : j + P]
+                turn(turned[:, b, :], [hp[:, t0 + r, a + j : a + j + P], low[:, r, j : j + P], top, top])
+            nc.scalar.activation(staged[:], turned[:], ACT.Copy, scale=0.5)
+            for b in range(4):
+                r, j = b // 2, P * (b % 2)
+                turn(back[:, r, j : j + P], [staged[:, b, :]])
+            round_pair(nc.scalar.copy, ob[c], t0, back[:])
+            res = sb("res%d" % unit, [P, 2, HALF], F32)
+            nc.scalar.copy(res[:], back[:])
+            nc.sync.dma_start(out_rows[:, t0 : t0 + 2, a : a + HALF], res[:])
+
+        def sum_on_vector(unit, lo, hi):
+            c, t0 = unit // 2, 2 * (unit % 2)
+            a = HALF * c
+            mix = sb("mix%d" % unit, [P, 2, HALF], F32)
+            res = sb("res%d" % unit, [P, 2, HALF], F32)
+            nc.vector.tensor_tensor(mix[:], hp[:, t0 : t0 + 2, a : a + HALF], lo[:], ALU.subtract)
             nc.vector.scalar_tensor_tensor(res[:], mix[:], 0.5, hi[:], ALU.mult, ALU.add)
-            nc.sync.dma_start(out_rows[:, :, a : a + w], res[:])
-            ob.append(sb("ob%d" % c, [P, w, PACK], BF16))
-            interleave(nc.vector.tensor_copy if c == len(PIECES) - 1 else nc.scalar.copy, ob[c], res)
+            nc.sync.dma_start(out_rows[:, t0 : t0 + 2, a : a + HALF], res[:])
+            round_pair(nc.vector.tensor_copy, ob[c], t0, res[:])
 
         def planes(c):
-            a, w = PIECES[c]
-            ow = sb("ow%d" % c, [P, w], U32)
-            nc.vector.quantize_mx(out=ow[:].bitcast(FP8X4), scales=os_[:, a : a + w], in_=ob[c][:].rearrange("p n t -> p (n t)"))
-            nc.sync.dma_start(out_words[:, a : a + w], ow[:].bitcast(I32))
+            a = HALF * c
+            ow = sb("ow%d" % c, [P, HALF], U32)
+            nc.vector.quantize_mx(out=ow[:].bitcast(FP8X4), scales=os_[:, a : a + HALF], in_=ob[c][:].rearrange("p n t -> p (n t)"))
+            nc.sync.dma_start(out_words[:, a : a + HALF], ow[:].bitcast(I32))
 
-        h_gathers(0)
-        combine(0)
-        h_gathers(1)
+        for unit in range(3):
+            sum_on_tensor(unit, *extremes(unit))
+        last = extremes(3)
         planes(0)
-        combine(1)
-        h_gathers(2)
+        sum_on_vector(3, *last)
         planes(1)
-        combine(2)
-        planes(2)
         for q in range(4):
             queue = nc.scalar if q % 2 else nc.sync
             queue.dma_start(out_2[0, 4 * q : 4 * q + 4, :].bitcast(I32), os_[32 * q : 32 * q + 4, :].bitcast(I32))

@@ -51,71 +51,77 @@ def tile_picked_twlsoftbrange_none_po_kernel(
             nc.gpsimd.memset(tile[:].bitcast(I32), 0)
             return tile
 
-        def deal_words(name, raw):
-            tile = sb(name, [P, H], I32)
+        def deal_words(name, raw, after=None):
+            tile = sb(name, [P, H], I32, tag=after)
             nc.vector.tensor_copy(tile[:].rearrange("p (t c i) -> p c t i", t=PACK, i=4), raw[:].rearrange("p (c i t) -> p c t i", t=PACK, i=4))
             return tile
 
-        def deal_scales(name, raw):
-            tile = sb(name, [P, H], U8)
+        def deal_scales(name, raw, after=None):
+            tile = sb(name, [P, H], U8, tag=after)
             nc.vector.tensor_copy(tile[:].rearrange("p (t c i) -> p c t i", t=PACK, i=16), raw[:].rearrange("p (c i t) -> p c t i", t=PACK, i=16))
             return tile
 
-        def pick(name, words, scales, lst, after=None):
-            w = sb(name + "_words", [P, S], U32, tag=after)
-            s = sb(name + "_scales", [P, S], U8)
-            nc.vector.tensor_copy(w[:], words[:].bitcast(U32).indirect(lst[:]))
-            nc.vector.tensor_copy(s[:], scales[:].indirect(lst[:]))
-            return w, s
+        def pick(name, dtype, table, lst, after=None):
+            tile = sb(name, [P, S], dtype, tag=after)
+            nc.vector.tensor_copy(tile[:], table.indirect(lst[:]))
+            return tile
 
         def cols(lst, start, width):
             return lst[:, start // 16 : (start + width) // 16]
 
-        def interleave(engine_copy, dst, src):
-            engine_copy(dst[:].rearrange("p (c i) t -> p c t i", i=4), src[:].rearrange("p t (c i) -> p c t i", i=4))
-
         xs = zeroed("xs", T)
         w2s_raw = zeroed("w2s_raw", H)
         w13s_raw = zeroed("w13s_raw", H)
+        ident = sb("ident", [P, P], F32)
+        make_identity(nc, ident[:])
+        gain = sb("gain", [P, PACK], F32)
+        nc.gpsimd.dma_start(gain[:], gn.rearrange("(p t) o -> p (t o)", t=PACK))
 
         two_l = load_list("two_l", two)
-        xw = load_words("xw", x_words, T, nc.scalar)
-        w2w_raw = load_words("w2w_raw", w2_words, H, nc.scalar)
-        load_scales(xs, 0, x_scales, nc.sync)
-        load_scales(w2s_raw, 0, w2_scales, nc.scalar)
         offs_l = load_list("offs_l", offs)
+        w2w_raw = load_words("w2w_raw", w2_words, H, nc.sync)
+        load_scales(xs, 0, x_scales, nc.sync)
+        xw = load_words("xw", x_words, T, nc.sync)
+        load_scales(w2s_raw, 0, w2_scales, nc.sync)
+        w1w_raw = load_words("w1w_raw", w1_words, H, nc.sync)
+        w3w_raw = load_words("w3w_raw", w3_words, H, nc.sync)
         n2_l = load_list("n2_l", n2)
+        load_scales(w13s_raw, 0, w1_scales, nc.sync)
+        load_scales(w13s_raw, 4, w3_scales, nc.sync)
         n1_l = load_list("n1_l", n1)
         n3_l = load_list("n3_l", n3)
         n4_l = load_list("n4_l", n4)
-        gain = sb("gain", [P, PACK], F32)
-        nc.gpsimd.dma_start(gain[:], gn.rearrange("(p t) o -> p (t o)", t=PACK))
-        load_scales(w13s_raw, 4, w3_scales, nc.gpsimd)
-        w1w_raw = load_words("w1w_raw", w1_words, H, nc.sync)
-        load_scales(w13s_raw, 0, w1_scales, nc.sync)
-        w3w_raw = load_words("w3w_raw", w3_words, H, nc.sync)
-        ident = sb("ident", [P, P], F32)
-        make_identity(nc, ident[:])
 
-        x2w, x2s = pick("x2", xw, xs, two_l)
         w2w = deal_words("w2w", w2w_raw)
+        x2s = pick("x2_scales", U8, xs[:], two_l)
+        x1s = pick("x1_scales", U8, xs[:], offs_l)
         w2s = deal_scales("w2s", w2s_raw)
+        x2w = pick("x2_words", U32, xw[:].bitcast(U32), two_l)
 
-        th, dg, yg = [], [], []
+        dg = [sb("dg%d" % t, [P, 2 * S], F32) for t in range(PACK)]
+        nc.vector.memset(dg[0][:, S:], 0.0)
+        th = [dg[t][:, S:] for t in range(1, PACK)] + [sb("th_last", [P, S], F32)[:]]
         for t in range(PACK):
             bank = psum.tile([P, S], F32, name="d_bank", tag="bank%d" % t)
             m = slice(P * t, P * (t + 1))
             nc.tensor.matmul_mx(out=bank[:], lhsT=w2w[:, m].bitcast(FP8X4), lhsT_scale=w2s[:, m],
                                 rhs=x2w[:].bitcast(FP8X4), rhs_scale=x2s[:], start=True, stop=True)
-            th.append(sb("th%d" % t, [P, S], F32))
-            dg.append(sb("dg%d" % t, [P, 2 * S], F32))
-            nc.vector.memset(dg[t][:, S:], 0.0)
-            nc.scalar.activation(th[t][:], bank[:], ACT.Tanh)
+            nc.scalar.activation(th[t], bank[:], ACT.Tanh)
             nc.scalar.activation(dg[t][:, :S], bank[:], ACT.Copy, scale=gain[:, t : t + 1])
 
-        x1w, x1s = pick("x1", xw, xs, offs_l, after="w2s_raw")
+        x1w = pick("x1_words", U32, xw[:].bitcast(U32), offs_l, after="w2s_raw")
         w1w = deal_words("w1w", w1w_raw)
-        w13s = deal_scales("w13s", w13s_raw)
+        w3w = deal_words("w3w", w3w_raw)
+
+        prod = []
+
+        def d_product(t, after=None):
+            prod.append(sb("prod%d" % t, [P, S], F32, tag=after))
+            nc.vector.tensor_tensor(prod[t][:], dg[t][:].indirect(n2_l[:]), th[t], ALU.mult)
+
+        d_product(0)
+        w13s = deal_scales("w13s", w13s_raw, after="dg0")
+        yg = []
         for t in range(PACK):
             bank = psum.tile([P, S], F32, name="y_bank", tag="bank%d" % (PACK + t))
             m = slice(P * t, P * (t + 1))
@@ -123,17 +129,15 @@ def tile_picked_twlsoftbrange_none_po_kernel(
                                 rhs=x1w[:].bitcast(FP8X4), rhs_scale=x1s[:], start=True, stop=True)
             yg.append(sb("yg%d" % t, [P, S], F32))
             nc.scalar.activation(yg[t][:], bank[:], ACT.Copy, scale=gain[:, t : t + 1])
-        w3w = deal_words("w3w", w3w_raw)
+        d_product(1, after="w13s_raw")
+        d_product(2)
+        d_product(3)
 
         hw = [sb("hw%d" % t, [P, S], F32) for t in range(PACK)]
         hp = sb("hp", [P, PACK, S], F32)
 
         def round_pair(engine_copy, dst, t0, src):
             engine_copy(dst[:, :, t0 : t0 + 2].rearrange("p (c i) t -> p c i t", i=4), src.rearrange("p t (c i) -> p c i t", i=4))
-
-        prod = [sb("prod%d" % t, [P, S], F32) for t in range(PACK)]
-        for t in range(PACK):
-            nc.vector.tensor_tensor(prod[t][:], dg[t][:].indirect(n2_l[:]), th[t][:], ALU.mult)
 
         def z_pair(c, t0, zb, engine_copy, tag):
             a = HALF * c
@@ -226,6 +230,7 @@ def tile_picked_twlsoftbrange_none_po_kernel(
             mix = sb("mix%d" % unit, [P, 2, HALF], F32)
             res = sb("res%d" % unit, [P, 2, HALF], F32)
             nc.vector.tensor_tensor(mix[:], hp[:, t0 : t0 + 2, a : a + HALF], lo[:], ALU.subtract)
+            planes(0)
             nc.vector.scalar_tensor_tensor(res[:], mix[:], 0.5, hi[:], ALU.mult, ALU.add)
             nc.sync.dma_start(out_rows[:, t0 : t0 + 2, a : a + HALF], res[:])
             round_pair(nc.vector.tensor_copy, ob[c], t0, res[:])
@@ -238,9 +243,7 @@ def tile_picked_twlsoftbrange_none_po_kernel(
 
         for unit in range(3):
             sum_on_tensor(unit, *extremes(unit))
-        last = extremes(3)
-        planes(0)
-        sum_on_vector(3, *last)
+        sum_on_vector(3, *extremes(3))
         planes(1)
         for q in range(4):
             queue = nc.scalar if q % 2 else nc.sync

@@ -76,18 +76,18 @@ def tile_picked_twlsoftbrange_none_po_kernel(
         make_identity(nc, ident[:])
         gain = sb("gain", [P, PACK], F32)
         nc.gpsimd.dma_start(gain[:], gn.rearrange("(p t) o -> p (t o)", t=PACK))
+        load_scales(w13s_raw, 4, w3_scales, nc.gpsimd)
 
         two_l = load_list("two_l", two)
-        offs_l = load_list("offs_l", offs)
         w2w_raw = load_words("w2w_raw", w2_words, H, nc.sync)
+        offs_l = load_list("offs_l", offs)
+        n2_l = load_list("n2_l", n2)
         load_scales(xs, 0, x_scales, nc.sync)
         xw = load_words("xw", x_words, T, nc.sync)
         load_scales(w2s_raw, 0, w2_scales, nc.sync)
         w1w_raw = load_words("w1w_raw", w1_words, H, nc.sync)
         w3w_raw = load_words("w3w_raw", w3_words, H, nc.sync)
-        n2_l = load_list("n2_l", n2)
         load_scales(w13s_raw, 0, w1_scales, nc.sync)
-        load_scales(w13s_raw, 4, w3_scales, nc.sync)
         n1_l = load_list("n1_l", n1)
         n3_l = load_list("n3_l", n3)
         n4_l = load_list("n4_l", n4)
@@ -111,7 +111,7 @@ def tile_picked_twlsoftbrange_none_po_kernel(
 
         x1w = pick("x1_words", U32, xw[:].bitcast(U32), offs_l, after="w2s_raw")
         w1w = deal_words("w1w", w1w_raw)
-        w3w = deal_words("w3w", w3w_raw)
+        w3w = deal_words("w3w", w3w_raw, after="w1w_raw")
 
         prod = []
 
@@ -119,7 +119,7 @@ def tile_picked_twlsoftbrange_none_po_kernel(
             prod.append(sb("prod%d" % t, [P, S], F32, tag=after))
             nc.vector.tensor_tensor(prod[t][:], dg[t][:].indirect(n2_l[:]), th[t], ALU.mult)
 
-        d_product(0)
+        d_product(0, after="w3w_raw")
         w13s = deal_scales("w13s", w13s_raw, after="dg0")
         yg = []
         for t in range(PACK):
@@ -130,8 +130,8 @@ def tile_picked_twlsoftbrange_none_po_kernel(
             yg.append(sb("yg%d" % t, [P, S], F32))
             nc.scalar.activation(yg[t][:], bank[:], ACT.Copy, scale=gain[:, t : t + 1])
         d_product(1, after="w13s_raw")
-        d_product(2)
-        d_product(3)
+        d_product(2, after="dg1")
+        d_product(3, after="dg2")
 
         hw = [sb("hw%d" % t, [P, S], F32) for t in range(PACK)]
         hp = sb("hp", [P, PACK, S], F32)
@@ -159,7 +159,7 @@ def tile_picked_twlsoftbrange_none_po_kernel(
                 nc.tensor.matmul_mx(out=bank[:, i, :], lhsT=w3w[:, m].bitcast(FP8X4), lhsT_scale=w13s[4:P, m],
                                     rhs=zq[0][:].bitcast(FP8X4), rhs_scale=zq[1][:], start=True, stop=True)
             for i, t in enumerate(rows):
-                nc.scalar.copy(hw[t][:, HALF * c : HALF * (c + 1)], bank[:, i, :])
+                nc.scalar.activation(hw[t][:, HALF * c : HALF * (c + 1)], bank[:, i, :], ACT.Copy, scale=-1.0)
             return bank
 
         def h_plain(c, rows, bank):
@@ -185,19 +185,19 @@ def tile_picked_twlsoftbrange_none_po_kernel(
         os_ = sb("out_scales", [P, S], U8)
         ob = [sb("ob%d" % c, [P, HALF, PACK], BF16) for c in range(2)]
 
-        def extremes(unit):
+        def extremes(unit, order):
             c, t0 = unit // 2, 2 * (unit % 2)
             a = HALF * c
             u = sb("u%d" % unit, [P, 2, HALF], F32)
             v = sb("v%d" % unit, [P, 2, HALF], F32)
             for t in range(t0, t0 + 2):
-                nc.vector.tensor_tensor(u[:, t - t0, :], hw[t][:].indirect(cols(n3_l, a, HALF)), hp[:, t, a : a + HALF], ALU.subtract)
-                nc.vector.tensor_tensor(v[:, t - t0, :], hw[t][:].indirect(cols(n4_l, a, HALF)), hp[:, t, a : a + HALF], ALU.subtract)
-            lo = sb("lo%d" % unit, [P, 2, HALF], F32)
-            hi = sb("hi%d" % unit, [P, 2, HALF], F32)
-            nc.vector.scalar_tensor_tensor(lo[:], u[:], 0.0, v[:], ALU.min, ALU.min)
-            nc.vector.scalar_tensor_tensor(hi[:], u[:], 0.0, v[:], ALU.max, ALU.max)
-            return lo, hi
+                nc.vector.tensor_tensor(u[:, t - t0, :], hw[t][:].indirect(cols(n3_l, a, HALF)), hp[:, t, a : a + HALF], ALU.add)
+                nc.vector.tensor_tensor(v[:, t - t0, :], hw[t][:].indirect(cols(n4_l, a, HALF)), hp[:, t, a : a + HALF], ALU.add)
+            found = {}
+            for name, op in order:
+                found[name] = sb("%s%d" % (name, unit), [P, 2, HALF], F32)
+                nc.vector.scalar_tensor_tensor(found[name][:], u[:], 0.0, v[:], op, op)
+            return found["lo"], found["hi"]
 
         def turn(dst, terms):
             for i, term in enumerate(terms):
@@ -209,12 +209,11 @@ def tile_picked_twlsoftbrange_none_po_kernel(
             turned = psum.tile([P, 4, P], F32, name="turned", tag="bank%d" % (5 + 2 * (unit % 2)))
             back = psum.tile([P, 2, HALF], F32, name="back", tag="bank%d" % (6 * (1 - unit % 2)))
             low = sb("low%d" % unit, [P, 2, HALF], F32, tag="low")
-            nc.scalar.activation(low[:], lo[:], ACT.Copy, scale=-1.0)
+            nc.scalar.activation(low[:], lo[:], ACT.Copy, scale=-2.0)
             staged = sb("staged%d" % unit, [P, 4, P], F32)
             for b in range(4):
                 r, j = b // 2, P * (b % 2)
-                top = hi[:, r, j : j + P]
-                turn(turned[:, b, :], [hp[:, t0 + r, a + j : a + j + P], low[:, r, j : j + P], top, top])
+                turn(turned[:, b, :], [hp[:, t0 + r, a + j : a + j + P], hi[:, r, j : j + P], low[:, r, j : j + P]])
             nc.scalar.activation(staged[:], turned[:], ACT.Copy, scale=0.5)
             for b in range(4):
                 r, j = b // 2, P * (b % 2)
@@ -229,9 +228,9 @@ def tile_picked_twlsoftbrange_none_po_kernel(
             a = HALF * c
             mix = sb("mix%d" % unit, [P, 2, HALF], F32)
             res = sb("res%d" % unit, [P, 2, HALF], F32)
-            nc.vector.tensor_tensor(mix[:], hp[:, t0 : t0 + 2, a : a + HALF], lo[:], ALU.subtract)
+            nc.vector.tensor_tensor(mix[:], hp[:, t0 : t0 + 2, a : a + HALF], hi[:], ALU.add)
             planes(0)
-            nc.vector.scalar_tensor_tensor(res[:], mix[:], 0.5, hi[:], ALU.mult, ALU.add)
+            nc.vector.scalar_tensor_tensor(res[:], mix[:], 0.5, lo[:], ALU.mult, ALU.subtract)
             nc.sync.dma_start(out_rows[:, t0 : t0 + 2, a : a + HALF], res[:])
             round_pair(nc.vector.tensor_copy, ob[c], t0, res[:])
 
@@ -241,9 +240,10 @@ def tile_picked_twlsoftbrange_none_po_kernel(
             nc.vector.quantize_mx(out=ow[:].bitcast(FP8X4), scales=os_[:, a : a + HALF], in_=ob[c][:].rearrange("p n t -> p (n t)"))
             nc.sync.dma_start(out_words[:, a : a + HALF], ow[:].bitcast(I32))
 
+        lo_first = (("lo", ALU.min), ("hi", ALU.max))
         for unit in range(3):
-            sum_on_tensor(unit, *extremes(unit))
-        sum_on_vector(3, *extremes(3))
+            sum_on_tensor(unit, *extremes(unit, lo_first))
+        sum_on_vector(3, *extremes(3, lo_first[::-1]))
         planes(1)
         for q in range(4):
             queue = nc.scalar if q % 2 else nc.sync

from contextlib import ExitStack

import concourse.mybir as mybir
from concourse.masks import make_identity

F32 = mybir.dt.float32
BF16 = mybir.dt.bfloat16
I32 = mybir.dt.int32
U32 = mybir.dt.uint32
U16 = mybir.dt.uint16
U8 = mybir.dt.uint8
FP8X4 = mybir.dt.float8_e4m3fn_x4
ALU = mybir.AluOpType
ACT = mybir.ActivationFunctionType

P = 128
PACK = 4
T, S, H = 2048, 512, 512
HALF = S // 2
FLOPS = 3 * 2 * 512 * 512 * 512


def tile_picked_twlsoftbrange_none_po_kernel(
    tc, x_words, x_scales, w1_words, w1_scales, w2_words, w2_scales, gn, w3_words, w3_scales,
    offs, two, n1, n2, n3, n4, out_0, out_1, out_2,
):
    nc = tc.nc
    with ExitStack() as ctx:
        keep = ctx.enter_context(tc.tile_pool(name="keep", bufs=1))
        psum = ctx.enter_context(tc.psum_pool(name="psum", bufs=1))

        def sb(name, shape, dtype, tag=None):
            return keep.tile(shape, dtype, name=name, tag=tag or name, align_bytes=64)

        def load_list(name, src):
            tile = keep.tile([P, S // 16], U16, name=name)
            nc.sync.dma_start(tile[:], src)
            return tile

        def load_words(name, src, width, queue):
            tile = sb(name, [P, width], I32)
            queue.dma_start(tile[:], src[0].rearrange("p n t -> p (n t)").bitcast(I32))
            return tile

        def load_scales(tile, first, src, queue):
            for q in range(4):
                queue.dma_start(tile[32 * q + first : 32 * q + first + 4, :].bitcast(I32), src[0, 4 * q : 4 * q + 4, :].bitcast(I32))

        def zeroed(name, width):
            tile = sb(name, [P, width], U8)
            nc.gpsimd.memset(tile[:].bitcast(I32), 0)
            return tile

        def deal_words(name, raw, after=None):
            tile = sb(name, [P, H], I32, tag=after)
            nc.vector.tensor_copy(tile[:].rearrange("p (t c i) -> p c t i", t=PACK, i=4), raw[:].rearrange("p (c i t) -> p c t i", t=PACK, i=4))
            return tile

        def deal_scales(name, raw, after=None):
            tile = sb(name, [P, H], U8, tag=after)
            nc.vector.tensor_copy(tile[:].rearrange("p (t c i) -> p c t i", t=PACK, i=16), raw[:].rearrange("p (c i t) -> p c t i", t=PACK, i=16))
            return tile

        def pick(name, dtype, table, lst, after=None):
            tile = sb(name, [P, S], dtype, tag=after)
            nc.vector.tensor_copy(tile[:], table.indirect(lst[:]))
            return tile

        def cols(lst, start, width):
            return lst[:, start // 16 : (start + width) // 16]

        xs = zeroed("xs", T)
        w2s_raw = zeroed("w2s_raw", H)
        w13s_raw = zeroed("w13s_raw", H)
        ident = sb("ident", [P, P], F32)
        make_identity(nc, ident[:])
        gain = sb("gain", [P, PACK], F32)
        nc.gpsimd.dma_start(gain[:], gn.rearrange("(p t) o -> p (t o)", t=PACK))
        load_scales(w13s_raw, 4, w3_scales, nc.gpsimd)

        two_l = load_list("two_l", two)
        w2w_raw = load_words("w2w_raw", w2_words, H, nc.sync)
        offs_l = load_list("offs_l", offs)
        n2_l = load_list("n2_l", n2)
        load_scales(xs, 0, x_scales, nc.sync)
        xw = load_words("xw", x_words, T, nc.sync)
        load_scales(w2s_raw, 0, w2_scales, nc.sync)
        w1w_raw = load_words("w1w_raw", w1_words, H, nc.sync)
        w3w_raw = load_words("w3w_raw", w3_words, H, nc.sync)
        load_scales(w13s_raw, 0, w1_scales, nc.sync)
        n1_l = load_list("n1_l", n1)
        n3_l = load_list("n3_l", n3)
        n4_l = load_list("n4_l", n4)

        w2w = deal_words("w2w", w2w_raw)
        x2s = pick("x2_scales", U8, xs[:], two_l)
        x1s = pick("x1_scales", U8, xs[:], offs_l)
        w2s = deal_scales("w2s", w2s_raw)
        x2w = pick("x2_words", U32, xw[:].bitcast(U32), two_l)

        dg = [sb("dg%d" % t, [P, 2 * S], F32) for t in range(PACK)]
        nc.vector.memset(dg[0][:, S:], 0.0)
        th = [dg[t][:, S:] for t in range(1, PACK)] + [sb("th_last", [P, S], F32)[:]]
        for t in range(PACK):
            bank = psum.tile([P, S], F32, name="d_bank", tag="bank%d" % t)
            m = slice(P * t, P * (t + 1))
            nc.tensor.matmul_mx(out=bank[:], lhsT=w2w[:, m].bitcast(FP8X4), lhsT_scale=w2s[:, m],
                                rhs=x2w[:].bitcast(FP8X4), rhs_scale=x2s[:], start=True, stop=True)
            nc.scalar.activation(th[t], bank[:], ACT.Tanh)
            nc.scalar.activation(dg[t][:, :S], bank[:], ACT.Copy, scale=gain[:, t : t + 1])

        x1w = pick("x1_words", U32, xw[:].bitcast(U32), offs_l, after="w2s_raw")
        w1w = deal_words("w1w", w1w_raw)
        w3w = deal_words("w3w", w3w_raw, after="w1w_raw")

        prod = []

        def d_product(t, after=None):
            prod.append(sb("prod%d" % t, [P, S], F32, tag=after))
            nc.vector.tensor_tensor(prod[t][:], dg[t][:].indirect(n2_l[:]), th[t], ALU.mult)

        d_product(0, after="w3w_raw")
        w13s = deal_scales("w13s", w13s_raw, after="dg0")
        yg = []
        for t in range(PACK):
            bank = psum.tile([P, S], F32, name="y_bank", tag="bank%d" % (PACK + t))
            m = slice(P * t, P * (t + 1))
            nc.tensor.matmul_mx(out=bank[:], lhsT=w1w[:, m].bitcast(FP8X4), lhsT_scale=w13s[:, m],
                                rhs=x1w[:].bitcast(FP8X4), rhs_scale=x1s[:], start=True, stop=True)
            yg.append(sb("yg%d" % t, [P, S], F32))
            nc.scalar.activation(yg[t][:], bank[:], ACT.Copy, scale=gain[:, t : t + 1])
        d_product(1, after="w13s_raw")
        d_product(2, after="dg1")
        d_product(3, after="dg2")

        hw = [sb("hw%d" % t, [P, S], F32) for t in range(PACK)]
        hp = sb("hp", [P, PACK, S], F32)

        def round_pair(engine_copy, dst, t0, src):
            engine_copy(dst[:, :, t0 : t0 + 2].rearrange("p (c i) t -> p c i t", i=4), src.rearrange("p t (c i) -> p c i t", i=4))

        def z_pair(c, t0, zb, engine_copy, tag):
            a = HALF * c
            z = sb("z%d_%d" % (c, t0), [P, 2, HALF], F32, tag=tag)
            for t in (t0, t0 + 1):
                nc.vector.tensor_tensor(z[:, t - t0, :], yg[t][:].indirect(cols(n1_l, a, HALF)), prod[t][:, a : a + HALF], ALU.subtract)
            round_pair(engine_copy, zb, t0, z[:])

        def quantised(c, zb):
            zw = sb("zw%d" % c, [P, HALF], U32)
            zs = sb("zs%d" % c, [P, HALF], U8)
            nc.vector.quantize_mx(out=zw[:].bitcast(FP8X4), scales=zs[:], in_=zb[:].rearrange("p n t -> p (n t)"))
            return zw, zs

        def h_rows(c, zq, rows, tag):
            bank = psum.tile([P, len(rows), HALF], F32, name="h_bank", tag=tag)
            for i, t in enumerate(rows):
                m = slice(P * t, P * (t + 1))
                nc.tensor.matmul_mx(out=bank[:, i, :], lhsT=w3w[:, m].bitcast(FP8X4), lhsT_scale=w13s[4:P, m],
                                    rhs=zq[0][:].bitcast(FP8X4), rhs_scale=zq[1][:], start=True, stop=True)
            for i, t in enumerate(rows):
                nc.scalar.activation(hw[t][:, HALF * c : HALF * (c + 1)], bank[:, i, :], ACT.Copy, scale=-1.0)
            return bank

        def h_plain(c, rows, bank):
            nc.scalar.copy(hp[:, rows[0] : rows[-1] + 1, HALF * c : HALF * (c + 1)], bank[:])

        zb0 = sb("zb0", [P, HALF, PACK], BF16, tag="zb0")
        zb1 = sb("zb1", [P, HALF, PACK], BF16)
        z_pair(0, 0, zb0, nc.scalar.copy, "z_low")
        z_pair(0, 2, zb0, nc.scalar.copy, "z_high")
        z_pair(1, 0, zb1, nc.scalar.copy, "z_low")
        zq0 = quantised(0, zb0)
        z_pair(1, 2, zb1, nc.vector.tensor_copy, "zb0")
        zq1 = quantised(1, zb1)
        h_plain(0, (0, 1), h_rows(0, zq0, (0, 1), "bank0"))
        left = h_rows(0, zq0, (2, 3), "bank1")
        right = [(rows, h_rows(1, zq1, rows, tag)) for rows, tag in (((0,), "bank2"), ((1,), "bank3"), ((2, 3), "bank4"))]
        h_plain(0, (2, 3), left)
        for rows, bank in right:
            h_plain(1, rows, bank)

        out_rows = out_0.rearrange("(p t) j -> p t j", t=PACK)
        out_words = out_1[0].rearrange("p n t -> p (n t)").bitcast(I32)
        os_ = sb("out_scales", [P, S], U8)
        ob = [sb("ob%d" % c, [P, HALF, PACK], BF16) for c in range(2)]

        def extremes(unit, order):
            c, t0 = unit // 2, 2 * (unit % 2)
            a = HALF * c
            u = sb("u%d" % unit, [P, 2, HALF], F32)
            v = sb("v%d" % unit, [P, 2, HALF], F32)
            for t in range(t0, t0 + 2):
                nc.vector.tensor_tensor(u[:, t - t0, :], hw[t][:].indirect(cols(n3_l, a, HALF)), hp[:, t, a : a + HALF], ALU.add)
                nc.vector.tensor_tensor(v[:, t - t0, :], hw[t][:].indirect(cols(n4_l, a, HALF)), hp[:, t, a : a + HALF], ALU.add)
            found = {}
            for name, op in order:
                found[name] = sb("%s%d" % (name, unit), [P, 2, HALF], F32)
                nc.vector.scalar_tensor_tensor(found[name][:], u[:], 0.0, v[:], op, op)
            return found["lo"], found["hi"]

        def turn(dst, terms):
            for i, term in enumerate(terms):
                nc.tensor.matmul(dst, term, ident[:], start=(i == 0), stop=(i == len(terms) - 1), is_transpose=True)

        def sum_on_tensor(unit, lo, hi):
            c, t0 = unit // 2, 2 * (unit % 2)
            a = HALF * c
            turned = psum.tile([P, 4, P], F32, name="turned", tag="bank%d" % (5 + 2 * (unit % 2)))
            back = psum.tile([P, 2, HALF], F32, name="back", tag="bank%d" % (6 * (1 - unit % 2)))
            low = sb("low%d" % unit, [P, 2, HALF], F32, tag="low")
            nc.scalar.activation(low[:], lo[:], ACT.Copy, scale=-2.0)
            staged = sb("staged%d" % unit, [P, 4, P], F32)
            for b in range(4):
                r, j = b // 2, P * (b % 2)
                turn(turned[:, b, :], [hp[:, t0 + r, a + j : a + j + P], hi[:, r, j : j + P], low[:, r, j : j + P]])
            nc.scalar.activation(staged[:], turned[:], ACT.Copy, scale=0.5)
            for b in range(4):
                r, j = b // 2, P * (b % 2)
                turn(back[:, r, j : j + P], [staged[:, b, :]])
            round_pair(nc.scalar.copy, ob[c], t0, back[:])
            res = sb("res%d" % unit, [P, 2, HALF], F32)
            nc.scalar.copy(res[:], back[:])
            nc.sync.dma_start(out_rows[:, t0 : t0 + 2, a : a + HALF], res[:])

        def sum_on_vector(unit, lo, hi):
            c, t0 = unit // 2, 2 * (unit % 2)
            a = HALF * c
            mix = sb("mix%d" % unit, [P, 2, HALF], F32)
            res = sb("res%d" % unit, [P, 2, HALF], F32)
            nc.vector.tensor_tensor(mix[:], hp[:, t0 : t0 + 2, a : a + HALF], hi[:], ALU.add)
            planes(0)
            nc.vector.scalar_tensor_tensor(res[:], mix[:], 0.5, lo[:], ALU.mult, ALU.subtract)
            nc.sync.dma_start(out_rows[:, t0 : t0 + 2, a : a + HALF], res[:])
            round_pair(nc.vector.tensor_copy, ob[c], t0, res[:])

        def planes(c):
            a = HALF * c
            ow = sb("ow%d" % c, [P, HALF], U32)
            nc.vector.quantize_mx(out=ow[:].bitcast(FP8X4), scales=os_[:, a : a + HALF], in_=ob[c][:].rearrange("p n t -> p (n t)"))
            nc.sync.dma_start(out_words[:, a : a + HALF], ow[:].bitcast(I32))

        lo_first = (("lo", ALU.min), ("hi", ALU.max))
        for unit in range(3):
            sum_on_tensor(unit, *extremes(unit, lo_first))
        sum_on_vector(3, *extremes(3, lo_first[::-1]))
        planes(1)
        for q in range(4):
            queue = nc.scalar if q % 2 else nc.sync
            queue.dma_start(out_2[0, 4 * q : 4 * q + 4, :].bitcast(I32), os_[32 * q : 32 * q + 4, :].bitcast(I32))
